import numpy as np
import ml_dtypes

BF16 = ml_dtypes.bfloat16


def bf(x):
    return np.asarray(x, np.float32).astype(BF16)


def f32(x):
    return np.asarray(x, np.float32)


def f64(x):
    return np.asarray(x).astype(np.float64)


def striped(idx):
    return np.tile(idx.reshape(-1, 16).T, (8, 1))


def rows(idx, k):
    return np.tile(idx, (k, 1))


K, S, V, N, M = 128, 256, 128, 128, 128


def setup_inputs():
    return {"base": f32(np.random.standard_normal((K, S))), "v": f32(np.random.standard_normal((K, V))), "w": bf(np.random.standard_normal((K, M)) / np.sqrt(K)), "b": f32(0.5 * np.random.standard_normal((M, 1))), "offs": striped(np.random.permutation(S)[:N])}


def reference(base, v, w, b, offs):
    idx = offs[:16].T.reshape(-1)
    x = f64(base).copy()
    np.put_along_axis(x, rows(idx, len(x)), 0.75 * f64(v) + 0.25, axis=1)
    y = f64(w).T @ x
    return np.maximum(y + f64(b), 0.0)

@@ -1,0 +1,37 @@
+import concourse.mybir as mybir
+
+BF16, F32, U16 = mybir.dt.bfloat16, mybir.dt.float32, mybir.dt.uint16
+MULT, ADD = mybir.AluOpType.mult, mybir.AluOpType.add
+RELU = mybir.ActivationFunctionType.Relu
+
+K, S, N, M = 128, 256, 128, 128
+FLOPS = 2 * K * S * M
+
+
+def tile_lookup_put_aff_relu_kernel(tc, base, v, w, b, offs, out):
+    nc = tc.nc
+    with (
+        tc.tile_pool(name="held", bufs=1) as held,
+        tc.psum_pool(name="psum", bufs=1) as psum,
+    ):
+        offsets = held.tile([K, N // 16], U16)
+        x = held.tile([K, S], F32)
+        values = held.tile([K, N], F32)
+        weights = held.tile([K, M], BF16)
+        bias = held.tile([M, 1], F32)
+
+        nc.sync.dma_start(offsets[:], offs)
+        nc.scalar.dma_start(values[:], v)
+        nc.sync.dma_start(x[:], base)
+        nc.scalar.dma_start(weights[:], w)
+        nc.sync.dma_start(bias[:], b)
+
+        nc.vector.tensor_scalar(x[:].indirect(offsets[:]), values[:], 0.75, 0.25, MULT, ADD)
+
+        x_bf16 = held.tile([K, S], BF16)
+        nc.vector.tensor_copy(x_bf16[:], x[:])
+        product = psum.tile([M, S], F32)
+        nc.tensor.matmul(product[:], weights[:], x_bf16[:])
+        result = held.tile([M, S], F32)
+        nc.scalar.activation(result[:], product[:], RELU, bias=bias[:])
+        nc.sync.dma_start(out, result[:])

@@ -1,8 +1,7 @@
 import concourse.mybir as mybir
 
 BF16, F32, U16 = mybir.dt.bfloat16, mybir.dt.float32, mybir.dt.uint16
-MULT, ADD = mybir.AluOpType.mult, mybir.AluOpType.add
-RELU = mybir.ActivationFunctionType.Relu
+MULT, ADD, MAX = mybir.AluOpType.mult, mybir.AluOpType.add, mybir.AluOpType.max
 
 K, S, N, M = 128, 256, 128, 128
 FLOPS = 2 * K * S * M
@@ -33,5 +32,5 @@ def tile_lookup_put_aff_relu_kernel(tc, base, v, w, b, offs, out):
         product = psum.tile([M, S], F32)
         nc.tensor.matmul(product[:], weights[:], x_bf16[:])
         result = held.tile([M, S], F32)
-        nc.scalar.activation(result[:], product[:], RELU, bias=bias[:])
+        nc.vector.tensor_scalar(result[:], product[:], bias[:], 0.0, ADD, MAX)
         nc.sync.dma_start(out, result[:])

@@ -19,9 +19,9 @@ def tile_lookup_put_aff_relu_kernel(tc, base, v, w, b, offs, out):
         weights = held.tile([K, M], BF16)
         bias = held.tile([M, 1], F32)
 
+        nc.scalar.dma_start(x[:], base)
         nc.sync.dma_start(offsets[:], offs)
-        nc.scalar.dma_start(values[:], v)
-        nc.sync.dma_start(x[:], base)
+        nc.sync.dma_start(values[:], v)
         nc.scalar.dma_start(weights[:], w)
         nc.sync.dma_start(bias[:], b)
 

import concourse.mybir as mybir

BF16, F32, U16 = mybir.dt.bfloat16, mybir.dt.float32, mybir.dt.uint16
MULT, ADD, MAX = mybir.AluOpType.mult, mybir.AluOpType.add, mybir.AluOpType.max

K, S, N, M = 128, 256, 128, 128
FLOPS = 2 * K * S * M


def tile_lookup_put_aff_relu_kernel(tc, base, v, w, b, offs, out):
    nc = tc.nc
    with (
        tc.tile_pool(name="held", bufs=1) as held,
        tc.psum_pool(name="psum", bufs=1) as psum,
    ):
        offsets = held.tile([K, N // 16], U16)
        x = held.tile([K, S], F32)
        values = held.tile([K, N], F32)
        weights = held.tile([K, M], BF16)
        bias = held.tile([M, 1], F32)

        nc.scalar.dma_start(x[:], base)
        nc.sync.dma_start(offsets[:], offs)
        nc.sync.dma_start(values[:], v)
        nc.scalar.dma_start(weights[:], w)
        nc.sync.dma_start(bias[:], b)

        nc.vector.tensor_scalar(x[:].indirect(offsets[:]), values[:], 0.75, 0.25, MULT, ADD)

        x_bf16 = held.tile([K, S], BF16)
        nc.vector.tensor_copy(x_bf16[:], x[:])
        product = psum.tile([M, S], F32)
        nc.tensor.matmul(product[:], weights[:], x_bf16[:])
        result = held.tile([M, S], F32)
        nc.vector.tensor_scalar(result[:], product[:], bias[:], 0.0, ADD, MAX)
        nc.sync.dma_start(out, result[:])
